import numpy as np, ml_dtypes
CORES = [26,28,98,100,106,108,122,124]
N = 8
C = 64
SIGN = [[1,1,1,1,1,1,1,1],[1,-1,1,-1,1,-1,1,-1],[1,1,-1,-1,1,1,-1,-1],[1,-1,-1,1,1,-1,-1,1],[1,1,1,1,-1,-1,-1,-1],[1,-1,1,-1,-1,1,-1,1],[1,1,-1,-1,-1,-1,1,1],[1,-1,-1,1,-1,1,1,-1]]
def setup_inputs(rng):
    return {"x": rng.standard_normal((N, 128, C), dtype=np.float32).astype(ml_dtypes.bfloat16)}
def setup_inputs_big(rng):
    d = setup_inputs(rng)
    for k in ("x",): d[k] = (d[k].astype(np.float32) * 1048576.0).astype(d[k].dtype)
    return d
def setup_inputs_small(rng):
    d = setup_inputs(rng)
    for k in ("x",): d[k] = (d[k].astype(np.float32) * (1 / 1048576.0)).astype(d[k].dtype)
    return d
def setup_inputs_apart(rng):
    d = setup_inputs(rng)
    f = (10.0 ** rng.permutation(np.linspace(-1.5, 1.5, N))).astype(np.float32).reshape(N, 1, 1)
    for k in ("x",): d[k] = (d[k].astype(np.float32) * f).astype(d[k].dtype)
    return d
def reference(x):
    X = x.astype(np.float64)
    y = np.stack([sum(SIGN[r][j] * X[j] for j in range(N)) for r in range(N)])
    return {"y": y.astype(ml_dtypes.bfloat16)}

@@ -1,0 +1,179 @@
+from concourse.bass import DstId, RemoteDMATransfer
+from concourse.mybir import AluOpType
+
+C = 64
+HELP_MIN = None
+
+SCRATCH = {
+    "xx": ("sbuf", [128, 2 * C], "bfloat16"),
+    "sd": ("sbuf", [128, 2 * C], "bfloat16"),
+    "land": ("sbuf", [128, 4 * C], "bfloat16"),
+    "acc": ("sbuf", [128, 3 * C], "bfloat16"),
+}
+SEMAPHORES = ["ld", "xa", "v0", "v1", "a0", "a1", "a2", "a3", "c0", "c1", "c2", "st", "snt"]
+
+
+def _bits(m):
+    return [e for e in range(m.bit_length()) if (m >> e) & 1]
+
+
+def _mask(es):
+    return sum(1 << e for e in es)
+
+
+def _plan(T, topo):
+    cores = list(T.cores)
+    sign = T.tables["SIGN"]
+    n = len(cores)
+    chips = []
+    for c in cores:
+        if topo.chip(c) not in chips:
+            chips.append(topo.chip(c))
+    mem = [[r for r in range(n) if topo.chip(cores[r]) == ch] for ch in chips]
+    need = {}
+    for r in range(n):
+        for k, (ja, jb) in enumerate(mem):
+            need[(r, k)] = (0 if sign[r][ja] == sign[r][jb] else 1, sign[r][ja])
+    every = range(topo.CHIPS * topo.CORES_PER_CHIP)
+    sends = {}
+    helpers = [[] for _ in chips]
+    for k, ch in enumerate(chips):
+        far = [r for r in range(n) if r not in mem[k]]
+        near = {}
+        for r in far:
+            near[r] = [cores[j] for j in mem[k]
+                       if topo.may_write(cores[j], cores[r]) and topo.die(cores[j]) == topo.die(cores[r])]
+        orphans = [r for r in far if not near[r]]
+        for r in far:
+            dst = cores[r]
+            if near[r]:
+                src = near[r][0]
+            elif HELP_MIN is not None and len(orphans) >= HELP_MIN:
+                src = [c for c in every if topo.chip(c) == ch and c not in cores
+                       and topo.die(c) == topo.die(dst) and topo.may_write(c, dst)][0]
+                if src not in helpers[k]:
+                    helpers[k].append(src)
+            else:
+                src = [cores[j] for j in mem[k] if topo.may_write(cores[j], dst)][0]
+            sends.setdefault(src, {}).setdefault(need[(r, k)][0], []).append(dst)
+    calls = {}
+    arrive = {}
+    for src, by in sends.items():
+        k = chips.index(topo.chip(src))
+        m = -1
+        for dsts in by.values():
+            for d in dsts:
+                m &= topo.mask(src, d)
+        eng = _bits(m)
+        w = sum(len(d) for d in by.values())
+        parts = []
+        if len(by) == 1:
+            parts = [(p, d, len(eng)) for p, d in by.items()]
+        elif len(eng) % w == 0:
+            per = len(eng) // w
+            for p in sorted(by):
+                d = list(by[p])
+                while d:
+                    size = 1 << (len(d).bit_length() - 1)
+                    parts.append((p, d[:size], per * size))
+                    d = d[size:]
+        else:
+            parts = [(p, by[p], len(eng) // len(by)) for p in sorted(by)]
+        out, at = [], 0
+        for p, d, ne in parts:
+            out.append((p, d, eng[at:at + ne]))
+            at += ne
+            for dst in d:
+                a, b = topo.chip(src), topo.chip(dst)
+                hops = 1 if (topo.mates(a, b) or topo.same_plane(a, b)) else 2
+                arrive[(dst, k)] = (ne, (src in helpers[k], len(d) / ne, hops))
+        calls[src] = out
+    return cores, chips, mem, need, helpers, calls, arrive
+
+
+def _send(g, T, topo, transfers):
+    ts = []
+    for src, dst, dsts, eng, sem in transfers:
+        ids = []
+        for d in dsts:
+            rid, pid, _ = topo.addr(d)
+            ids.append(DstId(rid=rid, pnc=pid))
+        ts.append(RemoteDMATransfer(dst_ids=ids, dma_engine_mask=_mask(eng), remote_sem=sem,
+                                    srcs=[src], dsts=[dst for _ in dsts], alu_op=0))
+    g.remote_dma_fused(ts, local_sem=T.sem.snt)
+    return sum(len(t[3]) for t in transfers)
+
+
+def rank_program(g, core, T, topo):
+    cores, chips, mem, need, helpers, calls, arrive = _plan(T, topo)
+    rank = T.rank_of(core)
+    if topo.chip(core) not in chips:
+        return
+    k = chips.index(topo.chip(core))
+    if rank is None and core not in helpers[k]:
+        return
+    sent = 0
+    mine = calls.get(core, [])
+
+    def step1_engines(c):
+        m = -1
+        for d in cores:
+            if d != c:
+                m &= topo.mask(c, d)
+        return _bits(m)
+
+    if rank is not None:
+        pos = mem[k].index(rank)
+        own = T.xx[:, pos * C:(pos + 1) * C]
+        g.sync.dma_start(out=own, in_=T.x[:]).then_inc(T.sem.ld, 16)
+        peers = [cores[j] for j in mem[k] if j != rank] + helpers[k]
+        g.wait_ge(T.sem.ld, 16)
+        sent += _send(g, T, topo, [(own, own, peers, step1_engines(core), T.sem.xa)])
+        g.vector.wait_ge(T.sem.ld, 16)
+    got = sum(len(step1_engines(cores[j])) for j in mem[k] if j != rank)
+    g.vector.wait_ge(T.sem.xa, got)
+
+    todo = []
+    for p, _, _ in mine:
+        if p not in todo:
+            todo.append(p)
+    if rank is not None and need[(rank, k)][0] not in todo:
+        todo.append(need[(rank, k)][0])
+    for p in todo:
+        g.vector.tensor_tensor(out=T.sd[:, p * C:(p + 1) * C], in0=T.xx[:, 0:C], in1=T.xx[:, C:2 * C],
+                               op=AluOpType.add if p == 0 else AluOpType.subtract).then_inc(T.sem["v%d" % p], 1)
+
+    if mine:
+        for p in todo:
+            if p in [q for q, _, _ in mine]:
+                g.wait_ge(T.sem["v%d" % p], 1)
+        slot = T.land[:, k * C:(k + 1) * C]
+        sent += _send(g, T, topo, [(T.sd[:, p * C:(p + 1) * C], slot, dsts, eng, T.sem["a%d" % k])
+                                   for p, dsts, eng in mine])
+
+    if rank is not None:
+        p, sg = need[(rank, k)]
+        cur = T.sd[:, p * C:(p + 1) * C]
+        g.vector.wait_ge(T.sem["v%d" % p], 1)
+        others = sorted([q for q in range(len(chips)) if q != k], key=lambda q: arrive[(core, q)][1])
+        for i, q in enumerate(others):
+            blk = T.land[:, q * C:(q + 1) * C]
+            sq = need[(rank, q)][1]
+            g.vector.wait_ge(T.sem["a%d" % q], arrive[(core, q)][0])
+            if i:
+                g.vector.wait_ge(T.sem["c%d" % (i - 1)], 1)
+            out = T.acc[:, i * C:(i + 1) * C]
+            if sg == sq:
+                in0, in1, op = cur, blk, AluOpType.add
+            elif sg > 0:
+                in0, in1, op = cur, blk, AluOpType.subtract
+            else:
+                in0, in1, op, sg = blk, cur, AluOpType.subtract, 1
+            g.vector.tensor_tensor(out=out, in0=in0, in1=in1, op=op).then_inc(T.sem["c%d" % i], 1)
+            cur = out
+        assert sg > 0
+        g.sync.wait_ge(T.sem["c%d" % (len(others) - 1)], 1)
+        g.sync.dma_start(out=T.y[:], in_=cur).then_inc(T.sem.st, 16)
+        g.sync.wait_ge(T.sem.st, 16)
+    if sent:
+        g.wait_ge(T.sem.snt, sent)

@@ -2,15 +2,21 @@ from concourse.bass import DstId, RemoteDMATransfer
 from concourse.mybir import AluOpType
 
 C = 64
-HELP_MIN = None
+H = 64
+F = 128
 
 SCRATCH = {
-    "xx": ("sbuf", [128, 2 * C], "bfloat16"),
-    "sd": ("sbuf", [128, 2 * C], "bfloat16"),
-    "land": ("sbuf", [128, 4 * C], "bfloat16"),
-    "acc": ("sbuf", [128, 3 * C], "bfloat16"),
+    "land": ("dram", [8, 128, C], "bfloat16"),
+    "z": ("sbuf", [128, 4 * F], "bfloat16"),
+    "zf": ("sbuf", [128, F], "bfloat16"),
+    "ones": ("sbuf", [128, 128], "bfloat16"),
+    "idn": ("sbuf", [128, 128], "bfloat16"),
+    "w": ("sbuf", [128, 4 * H], "bfloat16"),
+    "ysb": ("sbuf", [128, F], "bfloat16"),
+    "acc": ("psum", [128, F], "float32"),
 }
-SEMAPHORES = ["ld", "xa", "v0", "v1", "a0", "a1", "a2", "a3", "c0", "c1", "c2", "st", "snt"]
+SEMAPHORES = (["ld"] + ["e%d" % j for j in range(8)] + ["l%d" % j for j in range(8)]
+              + ["z0", "z1", "z2", "z3", "zf", "one", "idn", "w0", "w1", "w2", "w3", "mm", "fin", "st", "snt"])
 
 
 def _bits(m):
@@ -30,150 +36,196 @@ def _plan(T, topo):
         if topo.chip(c) not in chips:
             chips.append(topo.chip(c))
     mem = [[r for r in range(n) if topo.chip(cores[r]) == ch] for ch in chips]
-    need = {}
-    for r in range(n):
-        for k, (ja, jb) in enumerate(mem):
-            need[(r, k)] = (0 if sign[r][ja] == sign[r][jb] else 1, sign[r][ja])
-    every = range(topo.CHIPS * topo.CORES_PER_CHIP)
-    sends = {}
-    helpers = [[] for _ in chips]
-    for k, ch in enumerate(chips):
-        far = [r for r in range(n) if r not in mem[k]]
-        near = {}
-        for r in far:
-            near[r] = [cores[j] for j in mem[k]
-                       if topo.may_write(cores[j], cores[r]) and topo.die(cores[j]) == topo.die(cores[r])]
-        orphans = [r for r in far if not near[r]]
-        for r in far:
-            dst = cores[r]
-            if near[r]:
-                src = near[r][0]
-            elif HELP_MIN is not None and len(orphans) >= HELP_MIN:
-                src = [c for c in every if topo.chip(c) == ch and c not in cores
-                       and topo.die(c) == topo.die(dst) and topo.may_write(c, dst)][0]
-                if src not in helpers[k]:
-                    helpers[k].append(src)
+    other = {}
+    for a, b in mem:
+        other[a], other[b] = b, a
+    early = {j: [] for j in range(n)}
+    fold = {j: [] for j in range(n)}
+    relay = {j: [] for j in range(n)}
+    for pair in mem:
+        for r in range(n):
+            if r in pair:
+                continue
+            can = [j for j in pair if topo.may_write(cores[j], cores[r])]
+            if len(can) == 2:
+                for j in can:
+                    early[j].append(r)
             else:
-                src = [cores[j] for j in mem[k] if topo.may_write(cores[j], dst)][0]
-            sends.setdefault(src, {}).setdefault(need[(r, k)][0], []).append(dst)
-    calls = {}
-    arrive = {}
-    for src, by in sends.items():
-        k = chips.index(topo.chip(src))
+                a = can[0]
+                if sign[r][a] == sign[r][other[a]]:
+                    fold[a].append(r)
+                else:
+                    early[a].append(r)
+                    relay[a].append(r)
+    eng = {}
+    for j in range(n):
         m = -1
-        for dsts in by.values():
-            for d in dsts:
-                m &= topo.mask(src, d)
-        eng = _bits(m)
-        w = sum(len(d) for d in by.values())
-        parts = []
-        if len(by) == 1:
-            parts = [(p, d, len(eng)) for p, d in by.items()]
-        elif len(eng) % w == 0:
-            per = len(eng) // w
-            for p in sorted(by):
-                d = list(by[p])
-                while d:
-                    size = 1 << (len(d).bit_length() - 1)
-                    parts.append((p, d[:size], per * size))
-                    d = d[size:]
+        for d in range(n):
+            if d != j:
+                m &= topo.mask(cores[j], cores[d])
+        eng[j] = _bits(m)
+    first = {j: bool(fold[other[j]] or relay[other[j]]) for j in range(n)}
+
+    def hops(j, r):
+        a, b = topo.chip(cores[j]), topo.chip(cores[r])
+        return 1 if (topo.mates(a, b) or topo.same_plane(a, b)) else 2
+
+    calls = {}
+    blocks = {r: [] for r in range(n)}
+    near = {}
+    for j in range(n):
+        e = eng[j]
+        out = []
+        if first[j]:
+            few = e[::2][:4]
+            out.append((False, [("x", [other[j]], few)]))
+            near[other[j]] = len(few)
+            if early[j]:
+                out.append((False, [("x", list(early[j]), e)]))
         else:
-            parts = [(p, by[p], len(eng) // len(by)) for p in sorted(by)]
-        out, at = [], 0
-        for p, d, ne in parts:
-            out.append((p, d, eng[at:at + ne]))
-            at += ne
-            for dst in d:
-                a, b = topo.chip(src), topo.chip(dst)
-                hops = 1 if (topo.mates(a, b) or topo.same_plane(a, b)) else 2
-                arrive[(dst, k)] = (ne, (src in helpers[k], len(d) / ne, hops))
-        calls[src] = out
-    return cores, chips, mem, need, helpers, calls, arrive
-
-
-def _send(g, T, topo, transfers):
-    ts = []
-    for src, dst, dsts, eng, sem in transfers:
-        ids = []
-        for d in dsts:
-            rid, pid, _ = topo.addr(d)
-            ids.append(DstId(rid=rid, pnc=pid))
-        ts.append(RemoteDMATransfer(dst_ids=ids, dma_engine_mask=_mask(eng), remote_sem=sem,
-                                    srcs=[src], dsts=[dst for _ in dsts], alu_op=0))
-    g.remote_dma_fused(ts, local_sem=T.sem.snt)
-    return sum(len(t[3]) for t in transfers)
+            out.append((False, [("x", [other[j]] + early[j], e)]))
+            near[other[j]] = len(e)
+        for i, r in enumerate(early[j]):
+            blocks[r].append(((0, int(first[j]), i, hops(j, r)), j, "x", sign[r][j], len(e)))
+        late = [(kd, d) for kd, d in (("s", fold[j]), ("o", relay[j])) if d]
+        if late:
+            per = len(e) // len(late)
+            load = sum(len(d) for _, d in late)
+            out.append((True, [(kd, list(d), e[i * per:(i + 1) * per]) for i, (kd, d) in enumerate(late)]))
+            for kd, d in late:
+                for i, r in enumerate(d):
+                    sg = sign[r][j] if kd == "s" else sign[r][other[j]]
+                    blocks[r].append(((1, load, hops(j, r), i), j, kd, sg, per))
+        calls[j] = out
+    slot = {}
+    for r in range(n):
+        blocks[r].sort()
+        for i, b in enumerate(blocks[r]):
+            slot[(r, b[1], b[2])] = 2 + i
+    return cores, sign, other, calls, blocks, slot, near
 
 
 def rank_program(g, core, T, topo):
-    cores, chips, mem, need, helpers, calls, arrive = _plan(T, topo)
     rank = T.rank_of(core)
-    if topo.chip(core) not in chips:
+    if rank is None:
         return
-    k = chips.index(topo.chip(core))
-    if rank is None and core not in helpers[k]:
-        return
+    cores, sign, other, calls, blocks, slot, near = _plan(T, topo)
+    mate = other[rank]
+
+    g.sync.dma_start(out=T.land[0], in_=T.x[:]).then_inc(T.sem.ld, 16)
+    g.scalar.dma_start(out=T.z[0:H, 0:F], in_=T.x[:]).then_inc(T.sem.z0, 16)
+    g.vector.memset(T.ones[:], 1.0).then_inc(T.sem.one, 1)
+
+    g.wait_ge(T.sem.ld, 16)
     sent = 0
-    mine = calls.get(core, [])
+    for waits, transfers in calls[rank]:
+        if waits:
+            g.wait_ge(T.sem["e%d" % mate], near[rank])
+        ts = []
+        for kind, dsts, es in transfers:
+            ids, aps = [], []
+            for r in dsts:
+                rid, pid, _ = topo.addr(cores[r])
+                ids.append(DstId(rid=rid, pnc=pid))
+                aps.append(T.land[1 if r == mate else slot[(r, rank, kind)]])
+            ts.append(RemoteDMATransfer(
+                dst_ids=ids, dma_engine_mask=_mask(es), remote_sem=T.sem[("e%d" if kind == "x" else "l%d") % rank],
+                srcs=([T.land[0], T.land[1]] if kind == "s" else [T.land[0 if kind == "x" else 1]]),
+                dsts=aps, alu_op=(1 if kind == "s" else 0)))
+            sent += len(es)
+        g.remote_dma_fused(ts, local_sem=T.sem.snt)
 
-    def step1_engines(c):
-        m = -1
-        for d in cores:
-            if d != c:
-                m &= topo.mask(c, d)
-        return _bits(m)
+    g.wait_ge(T.sem.one, 1)
+    g.affine_select(out=T.idn[:], in_=T.ones[:], pattern=[[-1, 128]], compare_op=AluOpType.is_equal,
+                    fill=0.0, base=0, channel_multiplier=1).then_inc(T.sem.idn, 1)
 
-    if rank is not None:
-        pos = mem[k].index(rank)
-        own = T.xx[:, pos * C:(pos + 1) * C]
-        g.sync.dma_start(out=own, in_=T.x[:]).then_inc(T.sem.ld, 16)
-        peers = [cores[j] for j in mem[k] if j != rank] + helpers[k]
-        g.wait_ge(T.sem.ld, 16)
-        sent += _send(g, T, topo, [(own, own, peers, step1_engines(core), T.sem.xa)])
-        g.vector.wait_ge(T.sem.ld, 16)
-    got = sum(len(step1_engines(cores[j])) for j in mem[k] if j != rank)
-    g.vector.wait_ge(T.sem.xa, got)
+    bl = blocks[rank]
+    last = bl[-1]
+    rest = bl[:-1]
+    groups = [((sign[rank][rank], sign[rank][mate]), None)]
+    at = 0
+    if len(rest) % 2:
+        groups.append(((rest[0][3],), [2]))
+        at = 1
+    while at < len(rest):
+        groups.append(((rest[at][3], rest[at + 1][3]), [2 + at, 3 + at]))
+        at += 2
 
-    todo = []
-    for p, _, _ in mine:
-        if p not in todo:
-            todo.append(p)
-    if rank is not None and need[(rank, k)][0] not in todo:
-        todo.append(need[(rank, k)][0])
-    for p in todo:
-        g.vector.tensor_tensor(out=T.sd[:, p * C:(p + 1) * C], in0=T.xx[:, 0:C], in1=T.xx[:, C:2 * C],
-                               op=AluOpType.add if p == 0 else AluOpType.subtract).then_inc(T.sem["v%d" % p], 1)
+    def variant(sg, used):
+        if len(sg) == 2:
+            return (0 if sg[0] > 0 else 2) + (0 if sg[1] > 0 else 1)
+        lo = 0 if sg[0] > 0 else 2
+        return lo + 1 if (lo + 1 in used and lo not in used) else lo
 
-    if mine:
-        for p in todo:
-            if p in [q for q, _, _ in mine]:
-                g.wait_ge(T.sem["v%d" % p], 1)
-        slot = T.land[:, k * C:(k + 1) * C]
-        sent += _send(g, T, topo, [(T.sd[:, p * C:(p + 1) * C], slot, dsts, eng, T.sem["a%d" % k])
-                                   for p, dsts, eng in mine])
+    used = []
+    for sg, _ in groups:
+        if len(sg) == 2 and variant(sg, used) not in used:
+            used.append(variant(sg, used))
+    var = []
+    for sg, _ in groups:
+        v = variant(sg, used)
+        if v not in used:
+            used.append(v)
+        var.append(v)
 
-    if rank is not None:
-        p, sg = need[(rank, k)]
-        cur = T.sd[:, p * C:(p + 1) * C]
-        g.vector.wait_ge(T.sem["v%d" % p], 1)
-        others = sorted([q for q in range(len(chips)) if q != k], key=lambda q: arrive[(core, q)][1])
-        for i, q in enumerate(others):
-            blk = T.land[:, q * C:(q + 1) * C]
-            sq = need[(rank, q)][1]
-            g.vector.wait_ge(T.sem["a%d" % q], arrive[(core, q)][0])
-            if i:
-                g.vector.wait_ge(T.sem["c%d" % (i - 1)], 1)
-            out = T.acc[:, i * C:(i + 1) * C]
-            if sg == sq:
-                in0, in1, op = cur, blk, AluOpType.add
-            elif sg > 0:
-                in0, in1, op = cur, blk, AluOpType.subtract
-            else:
-                in0, in1, op, sg = blk, cur, AluOpType.subtract, 1
-            g.vector.tensor_tensor(out=out, in0=in0, in1=in1, op=op).then_inc(T.sem["c%d" % i], 1)
-            cur = out
-        assert sg > 0
-        g.sync.wait_ge(T.sem["c%d" % (len(others) - 1)], 1)
-        g.sync.dma_start(out=T.y[:], in_=cur).then_inc(T.sem.st, 16)
-        g.sync.wait_ge(T.sem.st, 16)
-    if sent:
-        g.wait_ge(T.sem.snt, sent)
+    def arrival(b):
+        return T.sem[("e%d" if b[2] == "x" else "l%d") % b[1]]
+
+    qs = [g.sync, g.scalar]
+    qi = 0
+    q = qs[qi]
+    q.wait_ge(T.sem["e%d" % mate], near[rank])
+    q.dma_start(out=T.z[H:2 * H, 0:F], in_=T.land[1]).then_inc(T.sem.z0, 16)
+    for i, (sg, sl) in enumerate(groups):
+        if sl is None:
+            continue
+        qi ^= 1
+        q = qs[qi]
+        for s in sl:
+            q.wait_ge(arrival(bl[s - 2]), bl[s - 2][4])
+        if len(sl) == 2:
+            q.dma_start(out=T.z[:, i * F:(i + 1) * F], in_=T.land[sl[0]:sl[1] + 1]).then_inc(T.sem["z%d" % i], 16)
+        else:
+            q.dma_start(out=T.z[0:H, i * F:(i + 1) * F], in_=T.land[sl[0]]).then_inc(T.sem["z%d" % i], 16)
+    qi ^= 1
+    q = qs[qi]
+    q.wait_ge(arrival(last), last[4])
+    q.dma_start(out=T.zf[0:H, :], in_=T.land[2 + len(rest)]).then_inc(T.sem.zf, 16)
+
+    left, right = T.idn[:, 0:H], T.idn[:, H:2 * H]
+    build = sorted(set(used) | ({0} if 3 in used else set()))
+    g.vector.wait_ge(T.sem.idn, 1)
+    for v in build:
+        out = T.w[:, v * H:(v + 1) * H]
+        if v == 0:
+            ins = g.vector.tensor_tensor(out=out, in0=left, in1=right, op=AluOpType.add)
+        elif v == 1:
+            ins = g.vector.tensor_tensor(out=out, in0=left, in1=right, op=AluOpType.subtract)
+        elif v == 2:
+            ins = g.vector.tensor_tensor(out=out, in0=right, in1=left, op=AluOpType.subtract)
+        else:
+            g.vector.wait_ge(T.sem.w0, 1)
+            ins = g.vector.tensor_scalar(out=out, in0=T.w[:, 0:H], scalar1=-1.0, scalar2=None, op0=AluOpType.mult)
+        ins.then_inc(T.sem["w%d" % v], 1)
+
+    seen = []
+    ins = None
+    for i, (sg, sl) in enumerate(groups):
+        v = var[i]
+        if v not in seen:
+            g.tensor.wait_ge(T.sem["w%d" % v], 1)
+            seen.append(v)
+        g.tensor.wait_ge(T.sem["z%d" % i], 32 if sl is None else 16)
+        kk = H * len(sg)
+        ins = g.tensor.matmul(out=T.acc[0:H, :], lhsT=T.w[0:kk, v * H:(v + 1) * H], rhs=T.z[0:kk, i * F:(i + 1) * F],
+                              start=(i == 0), stop=(i == len(groups) - 1))
+    ins.then_inc(T.sem.mm, 1)
+
+    g.vector.wait_ge(T.sem.mm, 1)
+    g.vector.wait_ge(T.sem.zf, 16)
+    g.vector.tensor_tensor(out=T.ysb[0:H, :], in0=T.acc[0:H, :], in1=T.zf[0:H, :],
+                           op=AluOpType.add if last[3] > 0 else AluOpType.subtract).then_inc(T.sem.fin, 1)
+    g.sync.wait_ge(T.sem.fin, 1)
+    g.sync.dma_start(out=T.y[:], in_=T.ysb[0:H, :]).then_inc(T.sem.st, 16)
+    g.sync.wait_ge(T.sem.st, 16)
+    g.wait_ge(T.sem.snt, sent)

@@ -2,21 +2,19 @@ from concourse.bass import DstId, RemoteDMATransfer
 from concourse.mybir import AluOpType
 
 C = 64
-H = 64
-F = 128
 
 SCRATCH = {
-    "land": ("dram", [8, 128, C], "bfloat16"),
-    "z": ("sbuf", [128, 4 * F], "bfloat16"),
-    "zf": ("sbuf", [128, F], "bfloat16"),
+    "xb": ("sbuf", [128, 8 * C], "bfloat16"),
+    "sb": ("sbuf", [128, 4 * C], "bfloat16"),
+    "sd": ("sbuf", [128, C], "bfloat16"),
     "ones": ("sbuf", [128, 128], "bfloat16"),
-    "idn": ("sbuf", [128, 128], "bfloat16"),
-    "w": ("sbuf", [128, 4 * H], "bfloat16"),
-    "ysb": ("sbuf", [128, F], "bfloat16"),
-    "acc": ("psum", [128, F], "float32"),
+    "idp": ("sbuf", [128, 128], "bfloat16"),
+    "idm": ("sbuf", [128, 128], "bfloat16"),
+    "ysb": ("sbuf", [128, C], "bfloat16"),
+    "acc": ("psum", [128, C], "float32"),
 }
-SEMAPHORES = (["ld"] + ["e%d" % j for j in range(8)] + ["l%d" % j for j in range(8)]
-              + ["z0", "z1", "z2", "z3", "zf", "one", "idn", "w0", "w1", "w2", "w3", "mm", "fin", "st", "snt"])
+SEMAPHORES = (["ld"] + ["e%d" % j for j in range(8)] + ["f%d" % k for k in range(4)]
+              + ["one", "ip", "im", "sv", "mm", "fin", "st", "snt"])
 
 
 def _bits(m):
@@ -36,35 +34,24 @@ def _plan(T, topo):
         if topo.chip(c) not in chips:
             chips.append(topo.chip(c))
     mem = [[r for r in range(n) if topo.chip(cores[r]) == ch] for ch in chips]
-    other = {}
-    for a, b in mem:
+    other, kof = {}, {}
+    for k, (a, b) in enumerate(mem):
         other[a], other[b] = b, a
+        kof[a] = kof[b] = k
     early = {j: [] for j in range(n)}
     fold = {j: [] for j in range(n)}
-    relay = {j: [] for j in range(n)}
     for pair in mem:
         for r in range(n):
             if r in pair:
                 continue
-            can = [j for j in pair if topo.may_write(cores[j], cores[r])]
-            if len(can) == 2:
-                for j in can:
-                    early[j].append(r)
+            dst = cores[r]
+            can = [j for j in pair if topo.may_write(cores[j], dst)]
+            near = [j for j in can if topo.die(cores[j]) == topo.die(dst)]
+            srv = near[0] if near else can[0]
+            if sign[r][pair[0]] == sign[r][pair[1]]:
+                fold[srv].append(r)
             else:
-                a = can[0]
-                if sign[r][a] == sign[r][other[a]]:
-                    fold[a].append(r)
-                else:
-                    early[a].append(r)
-                    relay[a].append(r)
-    eng = {}
-    for j in range(n):
-        m = -1
-        for d in range(n):
-            if d != j:
-                m &= topo.mask(cores[j], cores[d])
-        eng[j] = _bits(m)
-    first = {j: bool(fold[other[j]] or relay[other[j]]) for j in range(n)}
+                early[srv].append(r)
 
     def hops(j, r):
         a, b = topo.chip(cores[j]), topo.chip(cores[r])
@@ -72,160 +59,119 @@ def _plan(T, topo):
 
     calls = {}
     blocks = {r: [] for r in range(n)}
-    near = {}
     for j in range(n):
-        e = eng[j]
+        o = other[j]
+        early[j].sort(key=lambda r: -hops(j, r))
+        fold[j].sort(key=lambda r: -hops(j, r))
+        m = -1
+        for d in range(n):
+            if d != j:
+                m &= topo.mask(cores[j], cores[d])
+        e = _bits(m)
+        home = _bits(topo.mask(cores[j], cores[o]) & ~m)[:len(e) // 2]
+        load = 2 * len(early[j]) + len(fold[j])
         out = []
-        if first[j]:
-            few = e[::2][:4]
-            out.append((False, [("x", [other[j]], few)]))
-            near[other[j]] = len(few)
+        if fold[o] or early[o] or not early[j] or not home:
+            out.append((None, [("x", [o], e)]))
+            near = len(e)
             if early[j]:
-                out.append((False, [("x", list(early[j]), e)]))
+                out.append((None, [("x", list(early[j]), e)]))
         else:
-            out.append((False, [("x", [other[j]] + early[j], e)]))
-            near[other[j]] = len(e)
+            out.append((None, [("x", [o], home), ("x", list(early[j]), e)]))
+            near = len(home)
+        blocks[o].append(((0, 0, 0, 0), "x", j, sign[o][j], near))
         for i, r in enumerate(early[j]):
-            blocks[r].append(((0, int(first[j]), i, hops(j, r)), j, "x", sign[r][j], len(e)))
-        late = [(kd, d) for kd, d in (("s", fold[j]), ("o", relay[j])) if d]
-        if late:
-            per = len(e) // len(late)
-            load = sum(len(d) for _, d in late)
-            out.append((True, [(kd, list(d), e[i * per:(i + 1) * per]) for i, (kd, d) in enumerate(late)]))
-            for kd, d in late:
-                for i, r in enumerate(d):
-                    sg = sign[r][j] if kd == "s" else sign[r][other[j]]
-                    blocks[r].append(((1, load, hops(j, r), i), j, kd, sg, per))
+            blocks[r].append(((0, 1, i, hops(j, r)), "x", j, sign[r][j], len(e)))
+            blocks[r].append(((1, load, i, hops(j, r)), "x", o, sign[r][o], len(e)))
+        for i, r in enumerate(fold[j]):
+            blocks[r].append(((2, load, i, hops(j, r)), "s", kof[j], sign[r][j], len(e)))
+        if early[j]:
+            out.append(("e", [("o", list(early[j]), e)]))
+        if fold[j]:
+            out.append(("v", [("s", list(fold[j]), e)]))
         calls[j] = out
-    slot = {}
     for r in range(n):
         blocks[r].sort()
-        for i, b in enumerate(blocks[r]):
-            slot[(r, b[1], b[2])] = 2 + i
-    return cores, sign, other, calls, blocks, slot, near
+    return cores, sign, other, kof, calls, blocks
 
 
 def rank_program(g, core, T, topo):
     rank = T.rank_of(core)
     if rank is None:
         return
-    cores, sign, other, calls, blocks, slot, near = _plan(T, topo)
+    cores, sign, other, kof, calls, blocks = _plan(T, topo)
     mate = other[rank]
 
-    g.sync.dma_start(out=T.land[0], in_=T.x[:]).then_inc(T.sem.ld, 16)
-    g.scalar.dma_start(out=T.z[0:H, 0:F], in_=T.x[:]).then_inc(T.sem.z0, 16)
+    def xs(j):
+        return T.xb[:, j * C:(j + 1) * C]
+
+    def where(kind, i):
+        return xs(i) if kind == "x" else T.sb[:, i * C:(i + 1) * C]
+
+    def sem(kind, i):
+        return T.sem[("e%d" if kind == "x" else "f%d") % i]
+
+    mate_cnt = [b[4] for b in blocks[rank] if b[1] == "x" and b[2] == mate][0]
+
+    g.sync.dma_start(out=xs(rank), in_=T.x[:]).then_inc(T.sem.ld, 16)
     g.vector.memset(T.ones[:], 1.0).then_inc(T.sem.one, 1)
+    g.wait_ge(T.sem.one, 1)
+    g.affine_select(out=T.idp[:], in_=T.ones[:], pattern=[[-1, 128]], compare_op=AluOpType.is_equal,
+                    fill=0.0, base=0, channel_multiplier=1).then_inc(T.sem.ip, 1)
+    g.vector.wait_ge(T.sem.ip, 1)
+    g.vector.tensor_scalar(out=T.idm[:], in0=T.idp[:], scalar1=-1.0, scalar2=None,
+                           op0=AluOpType.mult).then_inc(T.sem.im, 1)
+
+    if any(w == "v" for w, _ in calls[rank]):
+        g.vector.wait_ge(T.sem.ld, 16)
+        g.vector.wait_ge(T.sem["e%d" % mate], mate_cnt)
+        g.vector.tensor_tensor(out=T.sd[:], in0=xs(rank), in1=xs(mate), op=AluOpType.add).then_inc(T.sem.sv, 1)
 
     g.wait_ge(T.sem.ld, 16)
     sent = 0
     for waits, transfers in calls[rank]:
-        if waits:
-            g.wait_ge(T.sem["e%d" % mate], near[rank])
+        if waits == "e":
+            g.wait_ge(T.sem["e%d" % mate], mate_cnt)
+        elif waits == "v":
+            g.wait_ge(T.sem.sv, 1)
         ts = []
         for kind, dsts, es in transfers:
-            ids, aps = [], []
+            ids = []
             for r in dsts:
                 rid, pid, _ = topo.addr(cores[r])
                 ids.append(DstId(rid=rid, pnc=pid))
-                aps.append(T.land[1 if r == mate else slot[(r, rank, kind)]])
-            ts.append(RemoteDMATransfer(
-                dst_ids=ids, dma_engine_mask=_mask(es), remote_sem=T.sem[("e%d" if kind == "x" else "l%d") % rank],
-                srcs=([T.land[0], T.land[1]] if kind == "s" else [T.land[0 if kind == "x" else 1]]),
-                dsts=aps, alu_op=(1 if kind == "s" else 0)))
+            if kind == "s":
+                src, dst, rs = T.sd[:], where("s", kof[rank]), sem("s", kof[rank])
+            elif kind == "x":
+                src, dst, rs = xs(rank), xs(rank), sem("x", rank)
+            else:
+                src, dst, rs = xs(mate), xs(mate), sem("x", mate)
+            ts.append(RemoteDMATransfer(dst_ids=ids, dma_engine_mask=_mask(es), remote_sem=rs,
+                                        srcs=[src], dsts=[dst for _ in dsts], alu_op=0))
             sent += len(es)
         g.remote_dma_fused(ts, local_sem=T.sem.snt)
 
-    g.wait_ge(T.sem.one, 1)
-    g.affine_select(out=T.idn[:], in_=T.ones[:], pattern=[[-1, 128]], compare_op=AluOpType.is_equal,
-                    fill=0.0, base=0, channel_multiplier=1).then_inc(T.sem.idn, 1)
-
     bl = blocks[rank]
+    todo = [(None, "x", rank, sign[rank][rank], 16)] + bl[:-1]
     last = bl[-1]
-    rest = bl[:-1]
-    groups = [((sign[rank][rank], sign[rank][mate]), None)]
-    at = 0
-    if len(rest) % 2:
-        groups.append(((rest[0][3],), [2]))
-        at = 1
-    while at < len(rest):
-        groups.append(((rest[at][3], rest[at + 1][3]), [2 + at, 3 + at]))
-        at += 2
-
-    def variant(sg, used):
-        if len(sg) == 2:
-            return (0 if sg[0] > 0 else 2) + (0 if sg[1] > 0 else 1)
-        lo = 0 if sg[0] > 0 else 2
-        return lo + 1 if (lo + 1 in used and lo not in used) else lo
-
-    used = []
-    for sg, _ in groups:
-        if len(sg) == 2 and variant(sg, used) not in used:
-            used.append(variant(sg, used))
-    var = []
-    for sg, _ in groups:
-        v = variant(sg, used)
-        if v not in used:
-            used.append(v)
-        var.append(v)
-
-    def arrival(b):
-        return T.sem[("e%d" if b[2] == "x" else "l%d") % b[1]]
-
-    qs = [g.sync, g.scalar]
-    qi = 0
-    q = qs[qi]
-    q.wait_ge(T.sem["e%d" % mate], near[rank])
-    q.dma_start(out=T.z[H:2 * H, 0:F], in_=T.land[1]).then_inc(T.sem.z0, 16)
-    for i, (sg, sl) in enumerate(groups):
-        if sl is None:
-            continue
-        qi ^= 1
-        q = qs[qi]
-        for s in sl:
-            q.wait_ge(arrival(bl[s - 2]), bl[s - 2][4])
-        if len(sl) == 2:
-            q.dma_start(out=T.z[:, i * F:(i + 1) * F], in_=T.land[sl[0]:sl[1] + 1]).then_inc(T.sem["z%d" % i], 16)
-        else:
-            q.dma_start(out=T.z[0:H, i * F:(i + 1) * F], in_=T.land[sl[0]]).then_inc(T.sem["z%d" % i], 16)
-    qi ^= 1
-    q = qs[qi]
-    q.wait_ge(arrival(last), last[4])
-    q.dma_start(out=T.zf[0:H, :], in_=T.land[2 + len(rest)]).then_inc(T.sem.zf, 16)
-
-    left, right = T.idn[:, 0:H], T.idn[:, H:2 * H]
-    build = sorted(set(used) | ({0} if 3 in used else set()))
-    g.vector.wait_ge(T.sem.idn, 1)
-    for v in build:
-        out = T.w[:, v * H:(v + 1) * H]
-        if v == 0:
-            ins = g.vector.tensor_tensor(out=out, in0=left, in1=right, op=AluOpType.add)
-        elif v == 1:
-            ins = g.vector.tensor_tensor(out=out, in0=left, in1=right, op=AluOpType.subtract)
-        elif v == 2:
-            ins = g.vector.tensor_tensor(out=out, in0=right, in1=left, op=AluOpType.subtract)
-        else:
-            g.vector.wait_ge(T.sem.w0, 1)
-            ins = g.vector.tensor_scalar(out=out, in0=T.w[:, 0:H], scalar1=-1.0, scalar2=None, op0=AluOpType.mult)
-        ins.then_inc(T.sem["w%d" % v], 1)
-
     seen = []
     ins = None
-    for i, (sg, sl) in enumerate(groups):
-        v = var[i]
-        if v not in seen:
-            g.tensor.wait_ge(T.sem["w%d" % v], 1)
-            seen.append(v)
-        g.tensor.wait_ge(T.sem["z%d" % i], 32 if sl is None else 16)
-        kk = H * len(sg)
-        ins = g.tensor.matmul(out=T.acc[0:H, :], lhsT=T.w[0:kk, v * H:(v + 1) * H], rhs=T.z[0:kk, i * F:(i + 1) * F],
-                              start=(i == 0), stop=(i == len(groups) - 1))
+    for i, (_, kind, idx, sg, cnt) in enumerate(todo):
+        if sg not in seen:
+            g.tensor.wait_ge(T.sem.ip if sg > 0 else T.sem.im, 1)
+            seen.append(sg)
+        g.tensor.wait_ge(T.sem.ld if i == 0 else sem(kind, idx), cnt)
+        ins = g.tensor.matmul(out=T.acc[:], lhsT=(T.idp[:] if sg > 0 else T.idm[:]), rhs=where(kind, idx),
+                              start=(i == 0), stop=(i == len(todo) - 1))
     ins.then_inc(T.sem.mm, 1)
+    if -1 not in seen:
+        g.tensor.wait_ge(T.sem.im, 1)
 
     g.vector.wait_ge(T.sem.mm, 1)
-    g.vector.wait_ge(T.sem.zf, 16)
-    g.vector.tensor_tensor(out=T.ysb[0:H, :], in0=T.acc[0:H, :], in1=T.zf[0:H, :],
+    g.vector.wait_ge(sem(last[1], last[2]), last[4])
+    g.vector.tensor_tensor(out=T.ysb[:], in0=T.acc[:], in1=where(last[1], last[2]),
                            op=AluOpType.add if last[3] > 0 else AluOpType.subtract).then_inc(T.sem.fin, 1)
     g.sync.wait_ge(T.sem.fin, 1)
-    g.sync.dma_start(out=T.y[:], in_=T.ysb[0:H, :]).then_inc(T.sem.st, 16)
+    g.sync.dma_start(out=T.y[:], in_=T.ysb[:]).then_inc(T.sem.st, 16)
     g.sync.wait_ge(T.sem.st, 16)
     g.wait_ge(T.sem.snt, sent)

@@ -2,19 +2,18 @@ from concourse.bass import DstId, RemoteDMATransfer
 from concourse.mybir import AluOpType
 
 C = 64
+P = 128
+UNIT = 8
 
 SCRATCH = {
     "xb": ("sbuf", [128, 8 * C], "bfloat16"),
-    "sb": ("sbuf", [128, 4 * C], "bfloat16"),
-    "sd": ("sbuf", [128, C], "bfloat16"),
-    "ones": ("sbuf", [128, 128], "bfloat16"),
-    "idp": ("sbuf", [128, 128], "bfloat16"),
-    "idm": ("sbuf", [128, 128], "bfloat16"),
+    "dd": ("sbuf", [128, P], "bfloat16"),
+    "idp": ("sbuf", [128, P], "bfloat16"),
+    "idm": ("sbuf", [128, P], "bfloat16"),
     "ysb": ("sbuf", [128, C], "bfloat16"),
     "acc": ("psum", [128, C], "float32"),
 }
-SEMAPHORES = (["ld"] + ["e%d" % j for j in range(8)] + ["f%d" % k for k in range(4)]
-              + ["one", "ip", "im", "sv", "mm", "fin", "st", "snt"])
+SEMAPHORES = ["ld"] + ["e%d" % j for j in range(8)] + ["cs", "own", "ip", "im", "mm", "fin", "st", "snt"]
 
 
 def _bits(m):
@@ -27,151 +26,156 @@ def _mask(es):
 
 def _plan(T, topo):
     cores = list(T.cores)
-    sign = T.tables["SIGN"]
     n = len(cores)
-    chips = []
-    for c in cores:
-        if topo.chip(c) not in chips:
-            chips.append(topo.chip(c))
-    mem = [[r for r in range(n) if topo.chip(cores[r]) == ch] for ch in chips]
-    other, kof = {}, {}
-    for k, (a, b) in enumerate(mem):
-        other[a], other[b] = b, a
-        kof[a] = kof[b] = k
-    early = {j: [] for j in range(n)}
-    fold = {j: [] for j in range(n)}
-    for pair in mem:
-        for r in range(n):
-            if r in pair:
-                continue
-            dst = cores[r]
-            can = [j for j in pair if topo.may_write(cores[j], dst)]
-            near = [j for j in can if topo.die(cores[j]) == topo.die(dst)]
-            srv = near[0] if near else can[0]
-            if sign[r][pair[0]] == sign[r][pair[1]]:
-                fold[srv].append(r)
-            else:
-                early[srv].append(r)
+    every = range(topo.CHIPS * topo.CORES_PER_CHIP)
 
-    def hops(j, r):
-        a, b = topo.chip(cores[j]), topo.chip(cores[r])
+    def hops(s, d):
+        a, b = topo.chip(s), topo.chip(d)
+        if a == b:
+            return 0
         return 1 if (topo.mates(a, b) or topo.same_plane(a, b)) else 2
 
-    calls = {}
-    blocks = {r: [] for r in range(n)}
-    for j in range(n):
-        o = other[j]
-        early[j].sort(key=lambda r: -hops(j, r))
-        fold[j].sort(key=lambda r: -hops(j, r))
+    def engines(s, dsts):
         m = -1
-        for d in range(n):
-            if d != j:
-                m &= topo.mask(cores[j], cores[d])
-        e = _bits(m)
-        home = _bits(topo.mask(cores[j], cores[o]) & ~m)[:len(e) // 2]
-        load = 2 * len(early[j]) + len(fold[j])
-        out = []
-        if fold[o] or early[o] or not early[j] or not home:
-            out.append((None, [("x", [o], e)]))
-            near = len(e)
-            if early[j]:
-                out.append((None, [("x", list(early[j]), e)]))
+        for d in dsts:
+            m &= topo.mask(s, d)
+        return _bits(m)
+
+    taken = set(cores)
+    other = {}
+    for j in range(n):
+        other[j] = [r for r in range(n) if r != j and topo.chip(cores[r]) == topo.chip(cores[j])][0]
+
+    queue = {}
+    aides = {}
+    arrive = {r: [] for r in range(n)}
+    ROW, HAND, HOP = 16, 40, 12
+    for j in range(n):
+        me = cores[j]
+        off = [r for r in range(n) if topo.chip(cores[r]) != topo.chip(me)]
+        far = sorted(off, key=lambda r: (-hops(me, cores[r]), (r - j) % n))
+        can = [r for r in far if topo.may_write(me, cores[r])]
+        half = len(off) // 2
+        if can:
+            keep = can[:half]
+            groups = [[r for r in far if r not in keep]]
         else:
-            out.append((None, [("x", [o], home), ("x", list(early[j]), e)]))
-            near = len(home)
-        blocks[o].append(((0, 0, 0, 0), "x", j, sign[o][j], near))
-        for i, r in enumerate(early[j]):
-            blocks[r].append(((0, 1, i, hops(j, r)), "x", j, sign[r][j], len(e)))
-            blocks[r].append(((1, load, i, hops(j, r)), "x", o, sign[r][o], len(e)))
-        for i, r in enumerate(fold[j]):
-            blocks[r].append(((2, load, i, hops(j, r)), "s", kof[j], sign[r][j], len(e)))
-        if early[j]:
-            out.append(("e", [("o", list(early[j]), e)]))
-        if fold[j]:
-            out.append(("v", [("s", list(fold[j]), e)]))
-        calls[j] = out
+            keep = []
+            groups = [far[0::2], far[1::2]]
+        mine = []
+        for grp in groups:
+            a = [c for c in every if c not in taken and topo.chip(c) == topo.chip(me) and topo.die(c) == topo.die(me)
+                 and all(topo.may_write(c, cores[r]) for r in grp)][0]
+            taken.add(a)
+            aides[a] = (j, grp)
+            mine.append(a)
+        queue[j] = mine + [cores[r] for r in keep] + [cores[other[j]]]
+        for i, a in enumerate(mine):
+            for k, r in enumerate(aides[a][1]):
+                arrive[r].append((ROW * (i + 1) + HAND + ROW * (k + 1) + HOP * hops(a, cores[r]), j))
+        for k, r in enumerate(keep):
+            arrive[r].append((ROW * (len(mine) + k + 1) + HOP * hops(me, cores[r]), j))
+        arrive[other[j]].append((ROW * len(queue[j]), j))
     for r in range(n):
-        blocks[r].sort()
-    return cores, sign, other, kof, calls, blocks
+        arrive[r].sort()
+
+    eng = {}
+    for j in range(n):
+        eng[cores[j]] = engines(cores[j], queue[j])
+    for a, (j, grp) in aides.items():
+        eng[a] = engines(a, [cores[r] for r in grp] + [cores[j], cores[other[j]]])
+
+    slices = {}
+    team = {}
+    for j in range(n):
+        ch = topo.chip(cores[j])
+        team[j] = sorted(c for c in list(cores) + list(aides) if topo.chip(c) == ch)
+        units = P // UNIT
+        c0 = 0
+        for i, c in enumerate(team[j]):
+            w = units // len(team[j]) + (1 if i >= len(team[j]) - units % len(team[j]) else 0)
+            slices[c] = (c0 * UNIT, w * UNIT, [r for r in (j, other[j]) if cores[r] != c])
+            c0 += w
+    return cores, other, queue, aides, arrive, eng, slices, team
+
+
+def _ids(topo, dsts):
+    out = []
+    for d in dsts:
+        rid, pid, _ = topo.addr(d)
+        out.append(DstId(rid=rid, pnc=pid))
+    return out
 
 
 def rank_program(g, core, T, topo):
+    cores, other, queue, aides, arrive, eng, slices, team = _plan(T, topo)
     rank = T.rank_of(core)
-    if rank is None:
+    if rank is None and core not in aides:
         return
-    cores, sign, other, kof, calls, blocks = _plan(T, topo)
-    mate = other[rank]
+    sign = T.tables["SIGN"]
+    es = eng[core]
 
     def xs(j):
         return T.xb[:, j * C:(j + 1) * C]
 
-    def where(kind, i):
-        return xs(i) if kind == "x" else T.sb[:, i * C:(i + 1) * C]
+    def send(src, dst, sem, dsts):
+        g.remote_dma_fused([RemoteDMATransfer(dst_ids=_ids(topo, dsts), dma_engine_mask=_mask(es), remote_sem=sem,
+                                              srcs=[src], dsts=[dst for _ in dsts], alu_op=0)],
+                           local_sem=T.sem.snt)
 
-    def sem(kind, i):
-        return T.sem[("e%d" if kind == "x" else "f%d") % i]
+    if rank is not None:
+        g.sync.dma_start(out=xs(rank), in_=T.x[:]).then_inc(T.sem.ld, 16)
 
-    mate_cnt = [b[4] for b in blocks[rank] if b[1] == "x" and b[2] == mate][0]
+    c0, w, to = slices[core]
+    piece = T.dd[:, c0:c0 + w]
+    g.iota(piece, pattern=[[-1, w]], base=-c0, channel_multiplier=1,
+           allow_small_or_imprecise_dtypes=True).then_inc(T.sem.own, 1)
+    g.wait_ge(T.sem.own, 1)
+    send(piece, piece, T.sem.cs, [cores[r] for r in to])
 
-    g.sync.dma_start(out=xs(rank), in_=T.x[:]).then_inc(T.sem.ld, 16)
-    g.vector.memset(T.ones[:], 1.0).then_inc(T.sem.one, 1)
-    g.wait_ge(T.sem.one, 1)
-    g.affine_select(out=T.idp[:], in_=T.ones[:], pattern=[[-1, 128]], compare_op=AluOpType.is_equal,
-                    fill=0.0, base=0, channel_multiplier=1).then_inc(T.sem.ip, 1)
-    g.vector.wait_ge(T.sem.ip, 1)
-    g.vector.tensor_scalar(out=T.idm[:], in0=T.idp[:], scalar1=-1.0, scalar2=None,
-                           op0=AluOpType.mult).then_inc(T.sem.im, 1)
-
-    if any(w == "v" for w, _ in calls[rank]):
-        g.vector.wait_ge(T.sem.ld, 16)
-        g.vector.wait_ge(T.sem["e%d" % mate], mate_cnt)
-        g.vector.tensor_tensor(out=T.sd[:], in0=xs(rank), in1=xs(mate), op=AluOpType.add).then_inc(T.sem.sv, 1)
+    if rank is None:
+        j, grp = aides[core]
+        g.wait_ge(T.sem["e%d" % j], len(eng[cores[j]]))
+        send(xs(j), xs(j), T.sem["e%d" % j], [cores[r] for r in grp])
+        g.wait_ge(T.sem.snt, 2 * len(es))
+        return
 
     g.wait_ge(T.sem.ld, 16)
-    sent = 0
-    for waits, transfers in calls[rank]:
-        if waits == "e":
-            g.wait_ge(T.sem["e%d" % mate], mate_cnt)
-        elif waits == "v":
-            g.wait_ge(T.sem.sv, 1)
-        ts = []
-        for kind, dsts, es in transfers:
-            ids = []
-            for r in dsts:
-                rid, pid, _ = topo.addr(cores[r])
-                ids.append(DstId(rid=rid, pnc=pid))
-            if kind == "s":
-                src, dst, rs = T.sd[:], where("s", kof[rank]), sem("s", kof[rank])
-            elif kind == "x":
-                src, dst, rs = xs(rank), xs(rank), sem("x", rank)
-            else:
-                src, dst, rs = xs(mate), xs(mate), sem("x", mate)
-            ts.append(RemoteDMATransfer(dst_ids=ids, dma_engine_mask=_mask(es), remote_sem=rs,
-                                        srcs=[src], dsts=[dst for _ in dsts], alu_op=0))
-            sent += len(es)
-        g.remote_dma_fused(ts, local_sem=T.sem.snt)
+    send(xs(rank), xs(rank), T.sem["e%d" % rank], queue[rank])
 
-    bl = blocks[rank]
-    todo = [(None, "x", rank, sign[rank][rank], 16)] + bl[:-1]
-    last = bl[-1]
-    seen = []
+    g.vector.wait_ge(T.sem.own, 1)
+    g.vector.wait_ge(T.sem.cs, sum(len(eng[c]) for c in team[rank] if c != core))
+    g.vector.tensor_scalar(out=T.idp[:], in0=T.dd[:], scalar1=0.0, scalar2=None,
+                           op0=AluOpType.is_equal).then_inc(T.sem.ip, 1)
+    g.vector.tensor_scalar(out=T.idm[:], in0=T.dd[:], scalar1=0.0, scalar2=-1.0,
+                           op0=AluOpType.is_equal, op1=AluOpType.mult).then_inc(T.sem.im, 1)
+
+    def count(j):
+        for a, (k, grp) in aides.items():
+            if k == j and rank in grp:
+                return len(eng[a])
+        return len(eng[cores[j]])
+
+    order = [j for _, j in arrive[rank]]
+    todo = [rank] + order[:-1]
+    last = order[-1]
+    g.tensor.wait_ge(T.sem.ip, 1)
+    g.tensor.wait_ge(T.sem.im, 1)
     ins = None
-    for i, (_, kind, idx, sg, cnt) in enumerate(todo):
-        if sg not in seen:
-            g.tensor.wait_ge(T.sem.ip if sg > 0 else T.sem.im, 1)
-            seen.append(sg)
-        g.tensor.wait_ge(T.sem.ld if i == 0 else sem(kind, idx), cnt)
-        ins = g.tensor.matmul(out=T.acc[:], lhsT=(T.idp[:] if sg > 0 else T.idm[:]), rhs=where(kind, idx),
+    for i, j in enumerate(todo):
+        if i == 0:
+            g.tensor.wait_ge(T.sem.ld, 16)
+        else:
+            g.tensor.wait_ge(T.sem["e%d" % j], count(j))
+        ins = g.tensor.matmul(out=T.acc[:], lhsT=(T.idp[:] if sign[rank][j] > 0 else T.idm[:]), rhs=xs(j),
                               start=(i == 0), stop=(i == len(todo) - 1))
     ins.then_inc(T.sem.mm, 1)
-    if -1 not in seen:
-        g.tensor.wait_ge(T.sem.im, 1)
 
     g.vector.wait_ge(T.sem.mm, 1)
-    g.vector.wait_ge(sem(last[1], last[2]), last[4])
-    g.vector.tensor_tensor(out=T.ysb[:], in0=T.acc[:], in1=where(last[1], last[2]),
-                           op=AluOpType.add if last[3] > 0 else AluOpType.subtract).then_inc(T.sem.fin, 1)
+    g.vector.wait_ge(T.sem["e%d" % last], count(last))
+    g.vector.tensor_tensor(out=T.ysb[:], in0=T.acc[:], in1=xs(last),
+                           op=AluOpType.add if sign[rank][last] > 0 else AluOpType.subtract).then_inc(T.sem.fin, 1)
     g.sync.wait_ge(T.sem.fin, 1)
     g.sync.dma_start(out=T.y[:], in_=T.ysb[:]).then_inc(T.sem.st, 16)
     g.sync.wait_ge(T.sem.st, 16)
-    g.wait_ge(T.sem.snt, sent)
+    g.wait_ge(T.sem.snt, 2 * len(es))

from concourse.bass import DstId, RemoteDMATransfer
from concourse.mybir import AluOpType

C = 64
P = 128
UNIT = 8

SCRATCH = {
    "xb": ("sbuf", [128, 8 * C], "bfloat16"),
    "dd": ("sbuf", [128, P], "bfloat16"),
    "idp": ("sbuf", [128, P], "bfloat16"),
    "idm": ("sbuf", [128, P], "bfloat16"),
    "ysb": ("sbuf", [128, C], "bfloat16"),
    "acc": ("psum", [128, C], "float32"),
}
SEMAPHORES = ["ld"] + ["e%d" % j for j in range(8)] + ["cs", "own", "ip", "im", "mm", "fin", "st", "snt"]


def _bits(m):
    return [e for e in range(m.bit_length()) if (m >> e) & 1]


def _mask(es):
    return sum(1 << e for e in es)


def _plan(T, topo):
    cores = list(T.cores)
    n = len(cores)
    every = range(topo.CHIPS * topo.CORES_PER_CHIP)

    def hops(s, d):
        a, b = topo.chip(s), topo.chip(d)
        if a == b:
            return 0
        return 1 if (topo.mates(a, b) or topo.same_plane(a, b)) else 2

    def engines(s, dsts):
        m = -1
        for d in dsts:
            m &= topo.mask(s, d)
        return _bits(m)

    taken = set(cores)
    other = {}
    for j in range(n):
        other[j] = [r for r in range(n) if r != j and topo.chip(cores[r]) == topo.chip(cores[j])][0]

    queue = {}
    aides = {}
    arrive = {r: [] for r in range(n)}
    ROW, HAND, HOP = 16, 40, 12
    for j in range(n):
        me = cores[j]
        off = [r for r in range(n) if topo.chip(cores[r]) != topo.chip(me)]
        far = sorted(off, key=lambda r: (-hops(me, cores[r]), (r - j) % n))
        can = [r for r in far if topo.may_write(me, cores[r])]
        half = len(off) // 2
        if can:
            keep = can[:half]
            groups = [[r for r in far if r not in keep]]
        else:
            keep = []
            groups = [far[0::2], far[1::2]]
        mine = []
        for grp in groups:
            a = [c for c in every if c not in taken and topo.chip(c) == topo.chip(me) and topo.die(c) == topo.die(me)
                 and all(topo.may_write(c, cores[r]) for r in grp)][0]
            taken.add(a)
            aides[a] = (j, grp)
            mine.append(a)
        queue[j] = mine + [cores[r] for r in keep] + [cores[other[j]]]
        for i, a in enumerate(mine):
            for k, r in enumerate(aides[a][1]):
                arrive[r].append((ROW * (i + 1) + HAND + ROW * (k + 1) + HOP * hops(a, cores[r]), j))
        for k, r in enumerate(keep):
            arrive[r].append((ROW * (len(mine) + k + 1) + HOP * hops(me, cores[r]), j))
        arrive[other[j]].append((ROW * len(queue[j]), j))
    for r in range(n):
        arrive[r].sort()

    eng = {}
    for j in range(n):
        eng[cores[j]] = engines(cores[j], queue[j])
    for a, (j, grp) in aides.items():
        eng[a] = engines(a, [cores[r] for r in grp] + [cores[j], cores[other[j]]])

    slices = {}
    team = {}
    for j in range(n):
        ch = topo.chip(cores[j])
        team[j] = sorted(c for c in list(cores) + list(aides) if topo.chip(c) == ch)
        units = P // UNIT
        c0 = 0
        for i, c in enumerate(team[j]):
            w = units // len(team[j]) + (1 if i >= len(team[j]) - units % len(team[j]) else 0)
            slices[c] = (c0 * UNIT, w * UNIT, [r for r in (j, other[j]) if cores[r] != c])
            c0 += w
    return cores, other, queue, aides, arrive, eng, slices, team


def _ids(topo, dsts):
    out = []
    for d in dsts:
        rid, pid, _ = topo.addr(d)
        out.append(DstId(rid=rid, pnc=pid))
    return out


def rank_program(g, core, T, topo):
    cores, other, queue, aides, arrive, eng, slices, team = _plan(T, topo)
    rank = T.rank_of(core)
    if rank is None and core not in aides:
        return
    sign = T.tables["SIGN"]
    es = eng[core]

    def xs(j):
        return T.xb[:, j * C:(j + 1) * C]

    def send(src, dst, sem, dsts):
        g.remote_dma_fused([RemoteDMATransfer(dst_ids=_ids(topo, dsts), dma_engine_mask=_mask(es), remote_sem=sem,
                                              srcs=[src], dsts=[dst for _ in dsts], alu_op=0)],
                           local_sem=T.sem.snt)

    if rank is not None:
        g.sync.dma_start(out=xs(rank), in_=T.x[:]).then_inc(T.sem.ld, 16)

    c0, w, to = slices[core]
    piece = T.dd[:, c0:c0 + w]
    g.iota(piece, pattern=[[-1, w]], base=-c0, channel_multiplier=1,
           allow_small_or_imprecise_dtypes=True).then_inc(T.sem.own, 1)
    g.wait_ge(T.sem.own, 1)
    send(piece, piece, T.sem.cs, [cores[r] for r in to])

    if rank is None:
        j, grp = aides[core]
        g.wait_ge(T.sem["e%d" % j], len(eng[cores[j]]))
        send(xs(j), xs(j), T.sem["e%d" % j], [cores[r] for r in grp])
        g.wait_ge(T.sem.snt, 2 * len(es))
        return

    g.wait_ge(T.sem.ld, 16)
    send(xs(rank), xs(rank), T.sem["e%d" % rank], queue[rank])

    g.vector.wait_ge(T.sem.own, 1)
    g.vector.wait_ge(T.sem.cs, sum(len(eng[c]) for c in team[rank] if c != core))
    g.vector.tensor_scalar(out=T.idp[:], in0=T.dd[:], scalar1=0.0, scalar2=None,
                           op0=AluOpType.is_equal).then_inc(T.sem.ip, 1)
    g.vector.tensor_scalar(out=T.idm[:], in0=T.dd[:], scalar1=0.0, scalar2=-1.0,
                           op0=AluOpType.is_equal, op1=AluOpType.mult).then_inc(T.sem.im, 1)

    def count(j):
        for a, (k, grp) in aides.items():
            if k == j and rank in grp:
                return len(eng[a])
        return len(eng[cores[j]])

    order = [j for _, j in arrive[rank]]
    todo = [rank] + order[:-1]
    last = order[-1]
    g.tensor.wait_ge(T.sem.ip, 1)
    g.tensor.wait_ge(T.sem.im, 1)
    ins = None
    for i, j in enumerate(todo):
        if i == 0:
            g.tensor.wait_ge(T.sem.ld, 16)
        else:
            g.tensor.wait_ge(T.sem["e%d" % j], count(j))
        ins = g.tensor.matmul(out=T.acc[:], lhsT=(T.idp[:] if sign[rank][j] > 0 else T.idm[:]), rhs=xs(j),
                              start=(i == 0), stop=(i == len(todo) - 1))
    ins.then_inc(T.sem.mm, 1)

    g.vector.wait_ge(T.sem.mm, 1)
    g.vector.wait_ge(T.sem["e%d" % last], count(last))
    g.vector.tensor_tensor(out=T.ysb[:], in0=T.acc[:], in1=xs(last),
                           op=AluOpType.add if sign[rank][last] > 0 else AluOpType.subtract).then_inc(T.sem.fin, 1)
    g.sync.wait_ge(T.sem.fin, 1)
    g.sync.dma_start(out=T.y[:], in_=T.ysb[:]).then_inc(T.sem.st, 16)
    g.sync.wait_ge(T.sem.st, 16)
    g.wait_ge(T.sem.snt, 2 * len(es))
